import numpy as np
import ml_dtypes


def mxq(x, axis, fmt="e4m3"):
    dtype, down = {"e4m3": (ml_dtypes.float8_e4m3fn, 7), "e5m2": (ml_dtypes.float8_e5m2, 14)}[fmt]
    v = np.moveaxis(np.asarray(x, np.float32).astype(ml_dtypes.bfloat16).astype(np.float64), axis, -1)
    blocks = v.reshape(v.shape[:-1] + (-1, 32))
    amax = np.abs(blocks).max(-1, keepdims=True)
    byte = np.maximum(np.where(amax > 0, np.frexp(amax)[1] - 1 + 127, 0) - down, 1)
    scale = np.exp2(byte - 127.0)
    codes = (blocks / scale).astype(np.float32).astype(dtype).astype(np.float64)
    return np.moveaxis((codes * scale).reshape(v.shape), -1, axis)


WIDE = False


def mx_kscale(k):
    if not WIDE:
        return np.ones(k)
    levels = np.array([10, -10, 5, -5, 0])
    if k % 512:
        return np.exp2(np.random.permutation(np.resize(levels, k // 32))).repeat(32)
    a = np.empty((k // 512, 16))
    for p in range(k // 512):
        a[p, :8] = np.random.permutation(np.resize(levels, 8))
        for g in range(8):
            far = levels[np.abs(levels - a[p, g]) >= 10]
            a[p, g + 8] = far[np.random.randint(len(far))]
    return np.exp2(a.ravel()).repeat(32)


def f64(x):
    return np.asarray(x).astype(np.float64)


def striped(idx):
    return np.tile(np.asarray(idx).reshape(-1, 16).T, (8, 1)).astype(np.uint16)


def unstriped(offs):
    return offs[:16].T.reshape(-1).astype(np.int64)


E2M1 = np.array([0.0, 0.5, 1.0, 1.5, 2.0, 3.0, 4.0, 6.0, -0.0, -0.5, -1.0, -1.5, -2.0, -3.0, -4.0, -6.0])


def pack_weight(w, fmt):
    k, n = w.shape
    w = f64(np.asarray(w, np.float32).astype(ml_dtypes.bfloat16)).reshape(k // 32, 32, n)
    amax = np.abs(w).max(1)
    if fmt == "e4m3":
        byte = np.frexp(amax)[1] - 1 + 127 - 7
    else:
        mant, ex = np.frexp(amax / 6.0)
        byte = np.where(mant > 0.5, ex, ex - 1) + 127
    byte = np.clip(np.where(amax > 0, byte, 1), 1, 254)
    scaled = (w * np.exp2(127.0 - byte)[:, None, :]).reshape(k, n).astype(np.float32)
    by_word = np.ascontiguousarray(scaled.reshape(k // 512, 128, 4, n).transpose(0, 1, 3, 2))
    if fmt == "e4m3":
        words = by_word.astype(ml_dtypes.float8_e4m3fn).view(np.uint8)
    else:
        c = by_word.astype(ml_dtypes.float4_e2m1fn).view(np.uint8) & 0xF
        words = (c[..., 0::2] | (c[..., 1::2] << 4)).reshape(k // 512, 128, 2 * n)
    return np.ascontiguousarray(words), np.ascontiguousarray(byte.astype(np.uint8).reshape(k // 512, 16, n))


def unpack_weight(words, scales, fmt):
    g, _, n = scales.shape
    words = np.ascontiguousarray(words).reshape(g, 128, n, -1)
    if fmt == "e4m3":
        vals = words.view(ml_dtypes.float8_e4m3fn).astype(np.float64)
    else:
        nib = np.empty((g, 128, n, 4), np.uint8)
        nib[..., 0::2] = words & 0xF
        nib[..., 1::2] = words >> 4
        vals = E2M1[nib]
    vals = vals * np.repeat(np.exp2(scales.astype(np.float64) - 127.0), 8, axis=1)[..., None]
    return vals.transpose(0, 1, 3, 2).reshape(g * 512, n)


B, N, T, D, NQ = 1, 512, 2048, 512, 256


def setup_inputs():
    n = np.random.standard_normal
    idx = np.random.permutation(T)[:B * N]
    s = mx_kscale(D)[:, None]
    kp = pack_weight(n((D, T)) / s, "e4m3")
    return {
        "qT": (n((B, D, NQ)) * s * (1.00 / np.sqrt(D))).astype(np.float32),
        "k_words": kp[0],
        "k_scales": kp[1],
        "bm": (n((B, NQ, N))).astype(np.float32),
        "offs": striped(idx),
    }


def reference(qT, k_words, k_scales, bm, offs):
    idx = unstriped(offs)
    pick = lambda x, which: x[:, which].reshape(x.shape[0], B, -1).transpose(1, 0, 2)
    k = unpack_weight(k_words, k_scales, "e4m3")
    kg = pick(k, idx)
    qq = mxq(f64(qT), 1, "e4m3")
    a = qq.transpose(0, 2, 1) @ kg
    mu = np.mean(a, axis=-1, keepdims=True)
    x = a - mu
    va = np.mean(np.square(x), axis=-1, keepdims=True)
    y = x / np.sqrt(va + 0.0001) + f64(bm)
    return y

@@ -1,0 +1,127 @@
+from contextlib import ExitStack
+
+import concourse.mybir as mybir
+
+D, T, N, NQ = 512, 2048, 512, 256
+EPS = 0.0001
+FLOPS = 2 * NQ * D * N
+
+F32 = mybir.dt.float32
+BF16 = mybir.dt.bfloat16
+I32 = mybir.dt.int32
+U32 = mybir.dt.uint32
+U16 = mybir.dt.uint16
+U8 = mybir.dt.uint8
+FP8X4 = mybir.dt.float8_e4m3fn_x4
+ALU = mybir.AluOpType
+ACT = mybir.ActivationFunctionType
+
+P = 128
+PACK = 4
+HALF = N // 2
+Q_TILES = NQ // P
+
+
+def tile_attend_nrm_z_topk_kernel(tc, qT, k_words, k_scales, bm, offs, out):
+    nc = tc.nc
+    with ExitStack() as ctx:
+        sb = ctx.enter_context(tc.tile_pool(name="sb", bufs=1))
+        psum = ctx.enter_context(tc.psum_pool(name="psum", bufs=1))
+
+        offsets = sb.tile([P, N // 16], U16, name="offsets")
+        nc.sync.dma_start(offsets[:], offs)
+
+        pool_scales = sb.tile([P, T // 4], I32, name="pool_scales", align_bytes=64)
+        nc.vector.memset(pool_scales[:], 0)
+
+        q_raw = sb.tile([P, PACK, NQ], F32, name="q_raw")
+        nc.sync.dma_start(out=q_raw[:], in_=qT[0].rearrange("(p j) q -> p j q", j=PACK))
+
+        scale_rows = k_scales[0].bitcast(I32)
+        for r in range(4):
+            nc.sync.dma_start(out=pool_scales[r:P:32, :], in_=scale_rows[r:16:4, :])
+
+        pool_words = sb.tile([P, T], I32, name="pool_words", align_bytes=64)
+        nc.sync.dma_start(out=pool_words[:], in_=k_words[0].rearrange("p t r -> p (t r)").bitcast(I32))
+
+        bm_sb = sb.tile([P, Q_TILES, N], F32, name="bm_sb")
+        nc.sync.dma_start(out=bm_sb[:], in_=bm[0].rearrange("(t p) n -> p t n", p=P))
+
+        q_bf = [sb.tile([P, P, PACK], BF16, name="q_bf%d" % t, align_bytes=64) for t in range(Q_TILES)]
+        q_codes = [sb.tile([P, P], U32, name="q_codes%d" % t, align_bytes=64) for t in range(Q_TILES)]
+        q_scales = [sb.tile([P, P], U8, name="q_scales%d" % t, align_bytes=64) for t in range(Q_TILES)]
+
+        def q_columns(t):
+            return q_raw[:, :, t * P : (t + 1) * P].rearrange("p j q -> p q j")
+
+        def quantize(t):
+            nc.vector.quantize_mx(
+                out=q_codes[t][:].bitcast(FP8X4),
+                scales=q_scales[t][:],
+                in_=q_bf[t][:].rearrange("p q j -> p (q j)"),
+            )
+
+        nc.vector.tensor_copy(out=q_bf[0][:], in_=q_columns(0))
+        nc.scalar.copy(out=q_bf[1][:], in_=q_columns(1))
+
+        key_scales = sb.tile([P, N], U8, name="key_scales", align_bytes=64)
+        nc.vector.tensor_copy(out=key_scales[:], in_=pool_scales[:].bitcast(U8).indirect(offsets[:]))
+        quantize(0)
+        quantize(1)
+
+        key_words = [sb.tile([P, HALF], U32, name="key_words%d" % h, align_bytes=64) for h in range(2)]
+        scores = [[psum.tile([P, HALF], F32, name="scores%d%d" % (t, h)) for h in range(2)] for t in range(Q_TILES)]
+        for h in range(2):
+            half_offsets = offsets[:, h * HALF // 16 : (h + 1) * HALF // 16]
+            nc.vector.tensor_copy(out=key_words[h][:], in_=pool_words[:].bitcast(U32).indirect(half_offsets))
+            for t in range(Q_TILES):
+                nc.tensor.matmul_mx(
+                    out=scores[t][h][:],
+                    lhsT=q_codes[t][:].bitcast(FP8X4),
+                    lhsT_scale=q_scales[t][:],
+                    rhs=key_words[h][:].bitcast(FP8X4),
+                    rhs_scale=key_scales[:, h * HALF : (h + 1) * HALF],
+                    start=True,
+                    stop=True,
+                )
+
+        stats = [sb.tile([P, 2, 6], F32, name="stats%d" % t) for t in range(Q_TILES)]
+        for h in range(2):
+            for t in range(Q_TILES):
+                nc.vector.bn_stats(out=stats[t][:, h, :], in_=scores[t][h][:])
+
+        mean_var = [sb.tile([P, 2], F32, name="mean_var%d" % t) for t in range(Q_TILES)]
+        rstd = [sb.tile([P, 1], F32, name="rstd%d" % t) for t in range(Q_TILES)]
+        neg_mean = [sb.tile([P, 1], F32, name="neg_mean%d" % t) for t in range(Q_TILES)]
+        centred = [[sb.tile([P, HALF], F32, name="centred%d%d" % (t, h)) for h in range(2)] for t in range(Q_TILES)]
+        result = [[sb.tile([P, HALF], F32, name="result%d%d" % (t, h)) for h in range(2)] for t in range(Q_TILES)]
+
+        for t in range(Q_TILES):
+            nc.vector.bn_aggr(out=mean_var[t][:], in_=stats[t][:].rearrange("p h s -> p (h s)"))
+            nc.scalar.activation(out=rstd[t][:], in_=mean_var[t][:, 1:2], func=ACT.Abs_reciprocal_sqrt, bias=EPS)
+
+        def negate(t):
+            nc.vector.tensor_scalar(
+                out=neg_mean[t][:], in0=mean_var[t][:, 0:1], scalar1=-1.0, scalar2=None, op0=ALU.mult
+            )
+
+        negate(0)
+        nc.vector.tensor_scalar(
+            out=centred[0][0][:], in0=scores[0][0][:], scalar1=mean_var[0][:, 0:1], scalar2=None, op0=ALU.subtract
+        )
+        negate(1)
+        for t, h in ((0, 1), (1, 0), (1, 1)):
+            nc.scalar.activation(out=centred[t][h][:], in_=scores[t][h][:], func=ACT.Identity, bias=neg_mean[t][:])
+
+        for t in range(Q_TILES):
+            for h in range(2):
+                cols = slice(h * HALF, (h + 1) * HALF)
+                nc.vector.scalar_tensor_tensor(
+                    out=result[t][h][:],
+                    in0=centred[t][h][:],
+                    scalar=rstd[t][:],
+                    in1=bm_sb[:, t, cols],
+                    op0=ALU.mult,
+                    op1=ALU.add,
+                )
+                nc.sync.dma_start(out=out[0, t * P : (t + 1) * P, cols], in_=result[t][h][:])

@@ -20,6 +20,9 @@ P = 128
 PACK = 4
 HALF = N // 2
 Q_TILES = NQ // P
+STORE_AFTER = ((0, 256), (0, 512), (1, 256), (1, 384), (1, 512))
+PIECES = ((0, 0, 256), (0, 256, 256), (1, 0, 128), (1, 128, 128), (1, 256, 128), (1, 384, 128))
+CENTRED_ON_VECTOR = ()
 
 
 def tile_attend_nrm_z_topk_kernel(tc, qT, k_words, k_scales, bm, offs, out):
@@ -28,31 +31,35 @@ def tile_attend_nrm_z_topk_kernel(tc, qT, k_words, k_scales, bm, offs, out):
         sb = ctx.enter_context(tc.tile_pool(name="sb", bufs=1))
         psum = ctx.enter_context(tc.psum_pool(name="psum", bufs=1))
 
+        q_rows = qT[0].rearrange("(p j) q -> p j q", j=PACK)
+        q_raw = [sb.tile([P, PACK, P], F32, name="q_raw%d" % t) for t in range(Q_TILES)]
+        nc.sync.dma_start(out=q_raw[0][:], in_=q_rows[:, :, 0:P])
+
         offsets = sb.tile([P, N // 16], U16, name="offsets")
         nc.sync.dma_start(offsets[:], offs)
 
         pool_scales = sb.tile([P, T // 4], I32, name="pool_scales", align_bytes=64)
         nc.vector.memset(pool_scales[:], 0)
-
-        q_raw = sb.tile([P, PACK, NQ], F32, name="q_raw")
-        nc.sync.dma_start(out=q_raw[:], in_=qT[0].rearrange("(p j) q -> p j q", j=PACK))
-
         scale_rows = k_scales[0].bitcast(I32)
-        for r in range(4):
-            nc.sync.dma_start(out=pool_scales[r:P:32, :], in_=scale_rows[r:16:4, :])
+        for r, queue in enumerate((nc.sync, nc.scalar, nc.sync, nc.scalar)):
+            queue.dma_start(out=pool_scales[r:P:32, :], in_=scale_rows[r:16:4, :])
 
         pool_words = sb.tile([P, T], I32, name="pool_words", align_bytes=64)
         nc.sync.dma_start(out=pool_words[:], in_=k_words[0].rearrange("p t r -> p (t r)").bitcast(I32))
+        nc.sync.dma_start(out=q_raw[1][:], in_=q_rows[:, :, P : 2 * P])
 
         bm_sb = sb.tile([P, Q_TILES, N], F32, name="bm_sb")
         nc.sync.dma_start(out=bm_sb[:], in_=bm[0].rearrange("(t p) n -> p t n", p=P))
 
-        q_bf = [sb.tile([P, P, PACK], BF16, name="q_bf%d" % t, align_bytes=64) for t in range(Q_TILES)]
+        warm = sb.tile([P, 1], F32, name="warm")
+        nc.scalar.activation(out=warm[:], in_=q_raw[0][:, 0, 0:1], func=ACT.Abs_reciprocal_sqrt, scale=0.0, bias=EPS)
+
+        q_bf = [
+            sb.tile([P, P, PACK], BF16, name="q_bf0", align_bytes=64),
+            sb.tile([P, P, PACK], BF16, name="q_bf1", align_bytes=64, tag="reused"),
+        ]
         q_codes = [sb.tile([P, P], U32, name="q_codes%d" % t, align_bytes=64) for t in range(Q_TILES)]
         q_scales = [sb.tile([P, P], U8, name="q_scales%d" % t, align_bytes=64) for t in range(Q_TILES)]
-
-        def q_columns(t):
-            return q_raw[:, :, t * P : (t + 1) * P].rearrange("p j q -> p q j")
 
         def quantize(t):
             nc.vector.quantize_mx(
@@ -61,22 +68,26 @@ def tile_attend_nrm_z_topk_kernel(tc, qT, k_words, k_scales, bm, offs, out):
                 in_=q_bf[t][:].rearrange("p q j -> p (q j)"),
             )
 
-        nc.vector.tensor_copy(out=q_bf[0][:], in_=q_columns(0))
-        nc.scalar.copy(out=q_bf[1][:], in_=q_columns(1))
+        nc.vector.tensor_scalar(
+            out=q_bf[0][:], in0=q_raw[0][:].rearrange("p j q -> p q j"), scalar1=-1.0, scalar2=None, op0=ALU.mult
+        )
+        quantize(0)
+        nc.scalar.activation(out=q_bf[1][:].rearrange("p (c i) j -> p c j i", i=4), in_=q_raw[1][:].rearrange("p j (c i) -> p c j i", i=4), func=ACT.Copy, scale=-1.0)
 
         key_scales = sb.tile([P, N], U8, name="key_scales", align_bytes=64)
         nc.vector.tensor_copy(out=key_scales[:], in_=pool_scales[:].bitcast(U8).indirect(offsets[:]))
-        quantize(0)
-        quantize(1)
 
         key_words = [sb.tile([P, HALF], U32, name="key_words%d" % h, align_bytes=64) for h in range(2)]
-        scores = [[psum.tile([P, HALF], F32, name="scores%d%d" % (t, h)) for h in range(2)] for t in range(Q_TILES)]
         for h in range(2):
             half_offsets = offsets[:, h * HALF // 16 : (h + 1) * HALF // 16]
             nc.vector.tensor_copy(out=key_words[h][:], in_=pool_words[:].bitcast(U32).indirect(half_offsets))
-            for t in range(Q_TILES):
+        quantize(1)
+
+        neg_scores = [[psum.tile([P, HALF], F32, name="neg_scores%d%d" % (t, h)) for h in range(2)] for t in range(Q_TILES)]
+        for t in range(Q_TILES):
+            for h in range(2):
                 nc.tensor.matmul_mx(
-                    out=scores[t][h][:],
+                    out=neg_scores[t][h][:],
                     lhsT=q_codes[t][:].bitcast(FP8X4),
                     lhsT_scale=q_scales[t][:],
                     rhs=key_words[h][:].bitcast(FP8X4),
@@ -85,43 +96,54 @@ def tile_attend_nrm_z_topk_kernel(tc, qT, k_words, k_scales, bm, offs, out):
                     stop=True,
                 )
 
-        stats = [sb.tile([P, 2, 6], F32, name="stats%d" % t) for t in range(Q_TILES)]
-        for h in range(2):
-            for t in range(Q_TILES):
-                nc.vector.bn_stats(out=stats[t][:, h, :], in_=scores[t][h][:])
-
+        stats = [
+            sb.tile([P, 2, 6], F32, name="stats0", align_bytes=64, tag="reused"),
+            sb.tile([P, 2, 6], F32, name="stats1", align_bytes=64),
+        ]
         mean_var = [sb.tile([P, 2], F32, name="mean_var%d" % t) for t in range(Q_TILES)]
         rstd = [sb.tile([P, 1], F32, name="rstd%d" % t) for t in range(Q_TILES)]
-        neg_mean = [sb.tile([P, 1], F32, name="neg_mean%d" % t) for t in range(Q_TILES)]
-        centred = [[sb.tile([P, HALF], F32, name="centred%d%d" % (t, h)) for h in range(2)] for t in range(Q_TILES)]
-        result = [[sb.tile([P, HALF], F32, name="result%d%d" % (t, h)) for h in range(2)] for t in range(Q_TILES)]
 
-        for t in range(Q_TILES):
+        def half_stats(t, h):
+            nc.vector.bn_stats(out=stats[t][:, h, :], in_=neg_scores[t][h][:])
+
+        def aggregate(t):
             nc.vector.bn_aggr(out=mean_var[t][:], in_=stats[t][:].rearrange("p h s -> p (h s)"))
-            nc.scalar.activation(out=rstd[t][:], in_=mean_var[t][:, 1:2], func=ACT.Abs_reciprocal_sqrt, bias=EPS)
 
-        def negate(t):
-            nc.vector.tensor_scalar(
-                out=neg_mean[t][:], in0=mean_var[t][:, 0:1], scalar1=-1.0, scalar2=None, op0=ALU.mult
-            )
+        half_stats(0, 0)
+        half_stats(0, 1)
+        aggregate(0)
+        half_stats(1, 0)
+        half_stats(1, 1)
+        aggregate(1)
 
-        negate(0)
-        nc.vector.tensor_scalar(
-            out=centred[0][0][:], in0=scores[0][0][:], scalar1=mean_var[0][:, 0:1], scalar2=None, op0=ALU.subtract
-        )
-        negate(1)
-        for t, h in ((0, 1), (1, 0), (1, 1)):
-            nc.scalar.activation(out=centred[t][h][:], in_=scores[t][h][:], func=ACT.Identity, bias=neg_mean[t][:])
-
-        for t in range(Q_TILES):
-            for h in range(2):
-                cols = slice(h * HALF, (h + 1) * HALF)
-                nc.vector.scalar_tensor_tensor(
-                    out=result[t][h][:],
-                    in0=centred[t][h][:],
-                    scalar=rstd[t][:],
-                    in1=bm_sb[:, t, cols],
-                    op0=ALU.mult,
-                    op1=ALU.add,
+        centred = []
+        for i, (t, start, width) in enumerate(PIECES):
+            if start == 0:
+                nc.scalar.activation(out=rstd[t][:], in_=mean_var[t][:, 1:2], func=ACT.Abs_reciprocal_sqrt, bias=EPS)
+            piece = sb.tile([P, width], F32, name="centred%d" % i)
+            source = neg_scores[t][start // HALF][:, start % HALF : start % HALF + width]
+            neg_mean = mean_var[t][:, 0:1]
+            if i in CENTRED_ON_VECTOR:
+                nc.vector.tensor_scalar(
+                    out=piece[:], in0=source, scalar1=neg_mean, scalar2=-1.0, op0=ALU.subtract, op1=ALU.mult
                 )
-                nc.sync.dma_start(out=out[0, t * P : (t + 1) * P, cols], in_=result[t][h][:])
+            else:
+                nc.scalar.activation(out=piece[:], in_=source, func=ACT.Identity, scale=-1.0, bias=neg_mean)
+            centred.append(piece)
+
+        result = [sb.tile([P, N], F32, name="result%d" % t) for t in range(Q_TILES)]
+        stored = 0
+        for i, (t, start, width) in enumerate(PIECES):
+            cols = slice(start, start + width)
+            nc.vector.scalar_tensor_tensor(
+                out=result[t][:, cols],
+                in0=centred[i][:],
+                scalar=rstd[t][:],
+                in1=bm_sb[:, t, cols],
+                op0=ALU.mult,
+                op1=ALU.add,
+            )
+            if (t, start + width) in STORE_AFTER:
+                run = slice(stored, start + width)
+                nc.sync.dma_start(out=out[0, t * P : (t + 1) * P, run], in_=result[t][:, run])
+                stored = (start + width) % N

@@ -41,7 +41,7 @@ def tile_attend_nrm_z_topk_kernel(tc, qT, k_words, k_scales, bm, offs, out):
         pool_scales = sb.tile([P, T // 4], I32, name="pool_scales", align_bytes=64)
         nc.vector.memset(pool_scales[:], 0)
         scale_rows = k_scales[0].bitcast(I32)
-        for r, queue in enumerate((nc.sync, nc.scalar, nc.sync, nc.scalar)):
+        for r, queue in enumerate((nc.scalar, nc.sync, nc.sync, nc.sync)):
             queue.dma_start(out=pool_scales[r:P:32, :], in_=scale_rows[r:16:4, :])
 
         pool_words = sb.tile([P, T], I32, name="pool_words", align_bytes=64)

@@ -31,31 +31,38 @@ def tile_attend_nrm_z_topk_kernel(tc, qT, k_words, k_scales, bm, offs, out):
         sb = ctx.enter_context(tc.tile_pool(name="sb", bufs=1))
         psum = ctx.enter_context(tc.psum_pool(name="psum", bufs=1))
 
-        q_rows = qT[0].rearrange("(p j) q -> p j q", j=PACK)
-        q_raw = [sb.tile([P, PACK, P], F32, name="q_raw%d" % t) for t in range(Q_TILES)]
-        nc.sync.dma_start(out=q_raw[0][:], in_=q_rows[:, :, 0:P])
-
         offsets = sb.tile([P, N // 16], U16, name="offsets")
         nc.sync.dma_start(offsets[:], offs)
 
-        pool_scales = sb.tile([P, T // 4], I32, name="pool_scales", align_bytes=64)
-        nc.vector.memset(pool_scales[:], 0)
-        scale_rows = k_scales[0].bitcast(I32)
-        for r, queue in enumerate((nc.scalar, nc.sync, nc.sync, nc.sync)):
-            queue.dma_start(out=pool_scales[r:P:32, :], in_=scale_rows[r:16:4, :])
+        pool_scales = sb.tile([P, T // 4], I32, name="pool_scales", align_bytes=64, tag="staging")
+        nc.sync.dma_start(out=pool_scales[112:P, :], in_=k_scales[0].bitcast(I32))
+        nc.vector.memset(pool_scales[0:96, :], 0)
+        nc.vector.memset(pool_scales[96:112, :], 0)
+        key_scales = sb.tile([P, N // 4], I32, name="key_scales", align_bytes=64)
+        nc.vector.memset(key_scales[:], 0)
+
+        warm = sb.tile([P, 1], F32, name="warm")
+        nc.vector.memset(warm[:], 1.0)
+        nc.scalar.activation(out=warm[:], in_=warm[:], func=ACT.Abs_reciprocal_sqrt)
+
+        q_rows = qT[0].rearrange("(p j) q -> p j q", j=PACK)
+        q_raw = [sb.tile([P, PACK, P], F32, name="q_raw%d" % t) for t in range(Q_TILES)]
+        nc.sync.dma_start(out=q_raw[0][:], in_=q_rows[:, :, 0:P])
 
         pool_words = sb.tile([P, T], I32, name="pool_words", align_bytes=64)
         nc.sync.dma_start(out=pool_words[:], in_=k_words[0].rearrange("p t r -> p (t r)").bitcast(I32))
         nc.sync.dma_start(out=q_raw[1][:], in_=q_rows[:, :, P : 2 * P])
 
-        bm_sb = sb.tile([P, Q_TILES, N], F32, name="bm_sb")
-        nc.sync.dma_start(out=bm_sb[:], in_=bm[0].rearrange("(t p) n -> p t n", p=P))
-
-        warm = sb.tile([P, 1], F32, name="warm")
-        nc.scalar.activation(out=warm[:], in_=q_raw[0][:, 0, 0:1], func=ACT.Abs_reciprocal_sqrt, scale=0.0, bias=EPS)
+        listed_scales = sb.tile([P, N], U8, name="listed_scales", align_bytes=64)
+        nc.vector.tensor_copy(out=listed_scales[:], in_=pool_scales[:].bitcast(U8).indirect(offsets[:]))
+        for quad in range(4):
+            nc.scalar.dma_start(
+                out=key_scales[32 * quad : 32 * quad + 4, :],
+                in_=listed_scales[112 + 4 * quad : 116 + 4 * quad, :].bitcast(I32),
+            )
 
         q_bf = [
-            sb.tile([P, P, PACK], BF16, name="q_bf0", align_bytes=64),
+            sb.tile([P, P, PACK], BF16, name="q_bf0", align_bytes=64, tag="staging"),
             sb.tile([P, P, PACK], BF16, name="q_bf1", align_bytes=64, tag="reused"),
         ]
         q_codes = [sb.tile([P, P], U32, name="q_codes%d" % t, align_bytes=64) for t in range(Q_TILES)]
@@ -72,10 +79,15 @@ def tile_attend_nrm_z_topk_kernel(tc, qT, k_words, k_scales, bm, offs, out):
             out=q_bf[0][:], in0=q_raw[0][:].rearrange("p j q -> p q j"), scalar1=-1.0, scalar2=None, op0=ALU.mult
         )
         quantize(0)
-        nc.scalar.activation(out=q_bf[1][:].rearrange("p (c i) j -> p c j i", i=4), in_=q_raw[1][:].rearrange("p j (c i) -> p c j i", i=4), func=ACT.Copy, scale=-1.0)
+        nc.scalar.activation(
+            out=q_bf[1][:].rearrange("p (c i) j -> p c j i", i=4),
+            in_=q_raw[1][:].rearrange("p j (c i) -> p c j i", i=4),
+            func=ACT.Copy,
+            scale=-1.0,
+        )
 
-        key_scales = sb.tile([P, N], U8, name="key_scales", align_bytes=64)
-        nc.vector.tensor_copy(out=key_scales[:], in_=pool_scales[:].bitcast(U8).indirect(offsets[:]))
+        bm_sb = sb.tile([P, Q_TILES, N], F32, name="bm_sb", align_bytes=64, tag="staging")
+        nc.sync.dma_start(out=bm_sb[:], in_=bm[0].rearrange("(t p) n -> p t n", p=P))
 
         key_words = [sb.tile([P, HALF], U32, name="key_words%d" % h, align_bytes=64) for h in range(2)]
         for h in range(2):
@@ -91,7 +103,7 @@ def tile_attend_nrm_z_topk_kernel(tc, qT, k_words, k_scales, bm, offs, out):
                     lhsT=q_codes[t][:].bitcast(FP8X4),
                     lhsT_scale=q_scales[t][:],
                     rhs=key_words[h][:].bitcast(FP8X4),
-                    rhs_scale=key_scales[:, h * HALF : (h + 1) * HALF],
+                    rhs_scale=key_scales[:].bitcast(U8)[:, h * HALF : (h + 1) * HALF],
                     start=True,
                     stop=True,
                 )

@@ -21,7 +21,7 @@ PACK = 4
 HALF = N // 2
 Q_TILES = NQ // P
 STORE_AFTER = ((0, 256), (0, 512), (1, 256), (1, 384), (1, 512))
-PIECES = ((0, 0, 256), (0, 256, 256), (1, 0, 128), (1, 128, 128), (1, 256, 128), (1, 384, 128))
+PIECES = ((0, 0, 128), (0, 128, 128), (0, 256, 256), (1, 0, 128), (1, 128, 128), (1, 256, 128), (1, 384, 128))
 CENTRED_ON_VECTOR = ()
 
 
@@ -35,7 +35,7 @@ def tile_attend_nrm_z_topk_kernel(tc, qT, k_words, k_scales, bm, offs, out):
         nc.sync.dma_start(offsets[:], offs)
 
         pool_scales = sb.tile([P, T // 4], I32, name="pool_scales", align_bytes=64, tag="staging")
-        nc.sync.dma_start(out=pool_scales[112:P, :], in_=k_scales[0].bitcast(I32))
+        nc.scalar.dma_start(out=pool_scales[112:P, :], in_=k_scales[0].bitcast(I32))
         nc.vector.memset(pool_scales[0:96, :], 0)
         nc.vector.memset(pool_scales[96:112, :], 0)
         key_scales = sb.tile([P, N // 4], I32, name="key_scales", align_bytes=64)
@@ -55,8 +55,8 @@ def tile_attend_nrm_z_topk_kernel(tc, qT, k_words, k_scales, bm, offs, out):
 
         listed_scales = sb.tile([P, N], U8, name="listed_scales", align_bytes=64)
         nc.vector.tensor_copy(out=listed_scales[:], in_=pool_scales[:].bitcast(U8).indirect(offsets[:]))
-        for quad in range(4):
-            nc.scalar.dma_start(
+        for quad, queue in enumerate((nc.sync, nc.scalar, nc.sync, nc.scalar)):
+            queue.dma_start(
                 out=key_scales[32 * quad : 32 * quad + 4, :],
                 in_=listed_scales[112 + 4 * quad : 116 + 4 * quad, :].bitcast(I32),
             )

@@ -41,10 +41,6 @@ def tile_attend_nrm_z_topk_kernel(tc, qT, k_words, k_scales, bm, offs, out):
         key_scales = sb.tile([P, N // 4], I32, name="key_scales", align_bytes=64)
         nc.vector.memset(key_scales[:], 0)
 
-        warm = sb.tile([P, 1], F32, name="warm")
-        nc.vector.memset(warm[:], 1.0)
-        nc.scalar.activation(out=warm[:], in_=warm[:], func=ACT.Abs_reciprocal_sqrt)
-
         q_rows = qT[0].rearrange("(p j) q -> p j q", j=PACK)
         q_raw = [sb.tile([P, PACK, P], F32, name="q_raw%d" % t) for t in range(Q_TILES)]
         nc.sync.dma_start(out=q_raw[0][:], in_=q_rows[:, :, 0:P])

@@ -18,11 +18,18 @@ ACT = mybir.ActivationFunctionType
 
 P = 128
 PACK = 4
+QUADRANT = 32
+QUADRANT_ROWS = 4
+SCALE_ROWS = D // 32
+LANDING = P - SCALE_ROWS
+LIST_GROUP = 16
+BN_STATS = 6
 HALF = N // 2
 Q_TILES = NQ // P
-STORE_AFTER = ((0, 256), (0, 512), (1, 256), (1, 384), (1, 512))
+NEIGHBOURS = 4
+
 PIECES = ((0, 0, 128), (0, 128, 128), (0, 256, 256), (1, 0, 128), (1, 128, 128), (1, 256, 128), (1, 384, 128))
-CENTRED_ON_VECTOR = ()
+STORE_AFTER = ((0, 256), (0, 512), (1, 256), (1, 384), (1, 512))
 
 
 def tile_attend_nrm_z_topk_kernel(tc, qT, k_words, k_scales, bm, offs, out):
@@ -31,14 +38,14 @@ def tile_attend_nrm_z_topk_kernel(tc, qT, k_words, k_scales, bm, offs, out):
         sb = ctx.enter_context(tc.tile_pool(name="sb", bufs=1))
         psum = ctx.enter_context(tc.psum_pool(name="psum", bufs=1))
 
-        offsets = sb.tile([P, N // 16], U16, name="offsets")
+        offsets = sb.tile([P, N // LIST_GROUP], U16, name="offsets")
         nc.sync.dma_start(offsets[:], offs)
 
-        pool_scales = sb.tile([P, T // 4], I32, name="pool_scales", align_bytes=64, tag="staging")
-        nc.scalar.dma_start(out=pool_scales[112:P, :], in_=k_scales[0].bitcast(I32))
-        nc.vector.memset(pool_scales[0:96, :], 0)
-        nc.vector.memset(pool_scales[96:112, :], 0)
-        key_scales = sb.tile([P, N // 4], I32, name="key_scales", align_bytes=64)
+        pool_scales = sb.tile([P, T // PACK], I32, name="pool_scales", align_bytes=64, tag="staging")
+        nc.scalar.dma_start(out=pool_scales[LANDING:P, :], in_=k_scales[0].bitcast(I32))
+        nc.vector.memset(pool_scales[0 : P - QUADRANT, :], 0)
+        nc.vector.memset(pool_scales[P - QUADRANT : LANDING, :], 0)
+        key_scales = sb.tile([P, N // PACK], I32, name="key_scales", align_bytes=64)
         nc.vector.memset(key_scales[:], 0)
 
         q_rows = qT[0].rearrange("(p j) q -> p j q", j=PACK)
@@ -51,10 +58,11 @@ def tile_attend_nrm_z_topk_kernel(tc, qT, k_words, k_scales, bm, offs, out):
 
         listed_scales = sb.tile([P, N], U8, name="listed_scales", align_bytes=64)
         nc.vector.tensor_copy(out=listed_scales[:], in_=pool_scales[:].bitcast(U8).indirect(offsets[:]))
-        for quad, queue in enumerate((nc.sync, nc.scalar, nc.sync, nc.scalar)):
+        for quad, queue in enumerate((nc.scalar, nc.sync, nc.sync, nc.sync)):
+            first_row = LANDING + QUADRANT_ROWS * quad
             queue.dma_start(
-                out=key_scales[32 * quad : 32 * quad + 4, :],
-                in_=listed_scales[112 + 4 * quad : 116 + 4 * quad, :].bitcast(I32),
+                out=key_scales[QUADRANT * quad : QUADRANT * quad + QUADRANT_ROWS, :],
+                in_=listed_scales[first_row : first_row + QUADRANT_ROWS, :].bitcast(I32),
             )
 
         q_bf = [
@@ -76,8 +84,8 @@ def tile_attend_nrm_z_topk_kernel(tc, qT, k_words, k_scales, bm, offs, out):
         )
         quantize(0)
         nc.scalar.activation(
-            out=q_bf[1][:].rearrange("p (c i) j -> p c j i", i=4),
-            in_=q_raw[1][:].rearrange("p j (c i) -> p c j i", i=4),
+            out=q_bf[1][:].rearrange("p (c i) j -> p c j i", i=NEIGHBOURS),
+            in_=q_raw[1][:].rearrange("p j (c i) -> p c j i", i=NEIGHBOURS),
             func=ACT.Copy,
             scale=-1.0,
         )
@@ -87,11 +95,13 @@ def tile_attend_nrm_z_topk_kernel(tc, qT, k_words, k_scales, bm, offs, out):
 
         key_words = [sb.tile([P, HALF], U32, name="key_words%d" % h, align_bytes=64) for h in range(2)]
         for h in range(2):
-            half_offsets = offsets[:, h * HALF // 16 : (h + 1) * HALF // 16]
+            half_offsets = offsets[:, h * HALF // LIST_GROUP : (h + 1) * HALF // LIST_GROUP]
             nc.vector.tensor_copy(out=key_words[h][:], in_=pool_words[:].bitcast(U32).indirect(half_offsets))
         quantize(1)
 
-        neg_scores = [[psum.tile([P, HALF], F32, name="neg_scores%d%d" % (t, h)) for h in range(2)] for t in range(Q_TILES)]
+        neg_scores = [
+            [psum.tile([P, HALF], F32, name="neg_scores%d%d" % (t, h)) for h in range(2)] for t in range(Q_TILES)
+        ]
         for t in range(Q_TILES):
             for h in range(2):
                 nc.tensor.matmul_mx(
@@ -105,24 +115,15 @@ def tile_attend_nrm_z_topk_kernel(tc, qT, k_words, k_scales, bm, offs, out):
                 )
 
         stats = [
-            sb.tile([P, 2, 6], F32, name="stats0", align_bytes=64, tag="reused"),
-            sb.tile([P, 2, 6], F32, name="stats1", align_bytes=64),
+            sb.tile([P, 2, BN_STATS], F32, name="stats0", align_bytes=64, tag="reused"),
+            sb.tile([P, 2, BN_STATS], F32, name="stats1", align_bytes=64),
         ]
         mean_var = [sb.tile([P, 2], F32, name="mean_var%d" % t) for t in range(Q_TILES)]
         rstd = [sb.tile([P, 1], F32, name="rstd%d" % t) for t in range(Q_TILES)]
-
-        def half_stats(t, h):
-            nc.vector.bn_stats(out=stats[t][:, h, :], in_=neg_scores[t][h][:])
-
-        def aggregate(t):
+        for t in range(Q_TILES):
+            for h in range(2):
+                nc.vector.bn_stats(out=stats[t][:, h, :], in_=neg_scores[t][h][:])
             nc.vector.bn_aggr(out=mean_var[t][:], in_=stats[t][:].rearrange("p h s -> p (h s)"))
-
-        half_stats(0, 0)
-        half_stats(0, 1)
-        aggregate(0)
-        half_stats(1, 0)
-        half_stats(1, 1)
-        aggregate(1)
 
         centred = []
         for i, (t, start, width) in enumerate(PIECES):
@@ -130,13 +131,7 @@ def tile_attend_nrm_z_topk_kernel(tc, qT, k_words, k_scales, bm, offs, out):
                 nc.scalar.activation(out=rstd[t][:], in_=mean_var[t][:, 1:2], func=ACT.Abs_reciprocal_sqrt, bias=EPS)
             piece = sb.tile([P, width], F32, name="centred%d" % i)
             source = neg_scores[t][start // HALF][:, start % HALF : start % HALF + width]
-            neg_mean = mean_var[t][:, 0:1]
-            if i in CENTRED_ON_VECTOR:
-                nc.vector.tensor_scalar(
-                    out=piece[:], in0=source, scalar1=neg_mean, scalar2=-1.0, op0=ALU.subtract, op1=ALU.mult
-                )
-            else:
-                nc.scalar.activation(out=piece[:], in_=source, func=ACT.Identity, scale=-1.0, bias=neg_mean)
+            nc.scalar.activation(out=piece[:], in_=source, func=ACT.Identity, scale=-1.0, bias=mean_var[t][:, 0:1])
             centred.append(piece)
 
         result = [sb.tile([P, N], F32, name="result%d" % t) for t in range(Q_TILES)]

@@ -42,7 +42,7 @@ def tile_attend_nrm_z_topk_kernel(tc, qT, k_words, k_scales, bm, offs, out):
         nc.sync.dma_start(offsets[:], offs)
 
         pool_scales = sb.tile([P, T // PACK], I32, name="pool_scales", align_bytes=64, tag="staging")
-        nc.scalar.dma_start(out=pool_scales[LANDING:P, :], in_=k_scales[0].bitcast(I32))
+        nc.sync.dma_start(out=pool_scales[LANDING:P, :], in_=k_scales[0].bitcast(I32))
         nc.vector.memset(pool_scales[0 : P - QUADRANT, :], 0)
         nc.vector.memset(pool_scales[P - QUADRANT : LANDING, :], 0)
         key_scales = sb.tile([P, N // PACK], I32, name="key_scales", align_bytes=64)
@@ -58,9 +58,9 @@ def tile_attend_nrm_z_topk_kernel(tc, qT, k_words, k_scales, bm, offs, out):
 
         listed_scales = sb.tile([P, N], U8, name="listed_scales", align_bytes=64)
         nc.vector.tensor_copy(out=listed_scales[:], in_=pool_scales[:].bitcast(U8).indirect(offsets[:]))
-        for quad, queue in enumerate((nc.scalar, nc.sync, nc.sync, nc.sync)):
+        for quad in range(P // QUADRANT):
             first_row = LANDING + QUADRANT_ROWS * quad
-            queue.dma_start(
+            nc.sync.dma_start(
                 out=key_scales[QUADRANT * quad : QUADRANT * quad + QUADRANT_ROWS, :],
                 in_=listed_scales[first_row : first_row + QUADRANT_ROWS, :].bitcast(I32),
             )

@@ -42,7 +42,7 @@ def tile_attend_nrm_z_topk_kernel(tc, qT, k_words, k_scales, bm, offs, out):
         nc.sync.dma_start(offsets[:], offs)
 
         pool_scales = sb.tile([P, T // PACK], I32, name="pool_scales", align_bytes=64, tag="staging")
-        nc.sync.dma_start(out=pool_scales[LANDING:P, :], in_=k_scales[0].bitcast(I32))
+        nc.scalar.dma_start(out=pool_scales[LANDING:P, :], in_=k_scales[0].bitcast(I32))
         nc.vector.memset(pool_scales[0 : P - QUADRANT, :], 0)
         nc.vector.memset(pool_scales[P - QUADRANT : LANDING, :], 0)
         key_scales = sb.tile([P, N // PACK], I32, name="key_scales", align_bytes=64)

@@ -28,8 +28,8 @@ HALF = N // 2
 Q_TILES = NQ // P
 NEIGHBOURS = 4
 
-PIECES = ((0, 0, 128), (0, 128, 128), (0, 256, 256), (1, 0, 128), (1, 128, 128), (1, 256, 128), (1, 384, 128))
-STORE_AFTER = ((0, 256), (0, 512), (1, 256), (1, 384), (1, 512))
+PIECES = ((0, 0, 128), (0, 128, 128), (0, 256, 256), (1, 0, 256), (1, 256, 128), (1, 384, 128))
+STORE_AFTER = ((0, 128), (0, 256), (0, 512), (1, 256), (1, 512))
 
 
 def tile_attend_nrm_z_topk_kernel(tc, qT, k_words, k_scales, bm, offs, out):

@@ -28,7 +28,7 @@ HALF = N // 2
 Q_TILES = NQ // P
 NEIGHBOURS = 4
 
-PIECES = ((0, 0, 128), (0, 128, 128), (0, 256, 256), (1, 0, 256), (1, 256, 128), (1, 384, 128))
+PIECES = ((0, 0, 128), (0, 128, 128), (0, 256, 128), (0, 384, 128), (1, 0, 128), (1, 128, 128), (1, 256, 128), (1, 384, 128))
 STORE_AFTER = ((0, 128), (0, 256), (0, 512), (1, 256), (1, 512))
 
 

from contextlib import ExitStack

import concourse.mybir as mybir

D, T, N, NQ = 512, 2048, 512, 256
EPS = 0.0001
FLOPS = 2 * NQ * D * N

F32 = mybir.dt.float32
BF16 = mybir.dt.bfloat16
I32 = mybir.dt.int32
U32 = mybir.dt.uint32
U16 = mybir.dt.uint16
U8 = mybir.dt.uint8
FP8X4 = mybir.dt.float8_e4m3fn_x4
ALU = mybir.AluOpType
ACT = mybir.ActivationFunctionType

P = 128
PACK = 4
QUADRANT = 32
QUADRANT_ROWS = 4
SCALE_ROWS = D // 32
LANDING = P - SCALE_ROWS
LIST_GROUP = 16
BN_STATS = 6
HALF = N // 2
Q_TILES = NQ // P
NEIGHBOURS = 4

PIECES = ((0, 0, 128), (0, 128, 128), (0, 256, 128), (0, 384, 128), (1, 0, 128), (1, 128, 128), (1, 256, 128), (1, 384, 128))
STORE_AFTER = ((0, 128), (0, 256), (0, 512), (1, 256), (1, 512))


def tile_attend_nrm_z_topk_kernel(tc, qT, k_words, k_scales, bm, offs, out):
    nc = tc.nc
    with ExitStack() as ctx:
        sb = ctx.enter_context(tc.tile_pool(name="sb", bufs=1))
        psum = ctx.enter_context(tc.psum_pool(name="psum", bufs=1))

        offsets = sb.tile([P, N // LIST_GROUP], U16, name="offsets")
        nc.sync.dma_start(offsets[:], offs)

        pool_scales = sb.tile([P, T // PACK], I32, name="pool_scales", align_bytes=64, tag="staging")
        nc.scalar.dma_start(out=pool_scales[LANDING:P, :], in_=k_scales[0].bitcast(I32))
        nc.vector.memset(pool_scales[0 : P - QUADRANT, :], 0)
        nc.vector.memset(pool_scales[P - QUADRANT : LANDING, :], 0)
        key_scales = sb.tile([P, N // PACK], I32, name="key_scales", align_bytes=64)
        nc.vector.memset(key_scales[:], 0)

        q_rows = qT[0].rearrange("(p j) q -> p j q", j=PACK)
        q_raw = [sb.tile([P, PACK, P], F32, name="q_raw%d" % t) for t in range(Q_TILES)]
        nc.sync.dma_start(out=q_raw[0][:], in_=q_rows[:, :, 0:P])

        pool_words = sb.tile([P, T], I32, name="pool_words", align_bytes=64)
        nc.sync.dma_start(out=pool_words[:], in_=k_words[0].rearrange("p t r -> p (t r)").bitcast(I32))
        nc.sync.dma_start(out=q_raw[1][:], in_=q_rows[:, :, P : 2 * P])

        listed_scales = sb.tile([P, N], U8, name="listed_scales", align_bytes=64)
        nc.vector.tensor_copy(out=listed_scales[:], in_=pool_scales[:].bitcast(U8).indirect(offsets[:]))
        for quad in range(P // QUADRANT):
            first_row = LANDING + QUADRANT_ROWS * quad
            nc.sync.dma_start(
                out=key_scales[QUADRANT * quad : QUADRANT * quad + QUADRANT_ROWS, :],
                in_=listed_scales[first_row : first_row + QUADRANT_ROWS, :].bitcast(I32),
            )

        q_bf = [
            sb.tile([P, P, PACK], BF16, name="q_bf0", align_bytes=64, tag="staging"),
            sb.tile([P, P, PACK], BF16, name="q_bf1", align_bytes=64, tag="reused"),
        ]
        q_codes = [sb.tile([P, P], U32, name="q_codes%d" % t, align_bytes=64) for t in range(Q_TILES)]
        q_scales = [sb.tile([P, P], U8, name="q_scales%d" % t, align_bytes=64) for t in range(Q_TILES)]

        def quantize(t):
            nc.vector.quantize_mx(
                out=q_codes[t][:].bitcast(FP8X4),
                scales=q_scales[t][:],
                in_=q_bf[t][:].rearrange("p q j -> p (q j)"),
            )

        nc.vector.tensor_scalar(
            out=q_bf[0][:], in0=q_raw[0][:].rearrange("p j q -> p q j"), scalar1=-1.0, scalar2=None, op0=ALU.mult
        )
        quantize(0)
        nc.scalar.activation(
            out=q_bf[1][:].rearrange("p (c i) j -> p c j i", i=NEIGHBOURS),
            in_=q_raw[1][:].rearrange("p j (c i) -> p c j i", i=NEIGHBOURS),
            func=ACT.Copy,
            scale=-1.0,
        )

        bm_sb = sb.tile([P, Q_TILES, N], F32, name="bm_sb", align_bytes=64, tag="staging")
        nc.sync.dma_start(out=bm_sb[:], in_=bm[0].rearrange("(t p) n -> p t n", p=P))

        key_words = [sb.tile([P, HALF], U32, name="key_words%d" % h, align_bytes=64) for h in range(2)]
        for h in range(2):
            half_offsets = offsets[:, h * HALF // LIST_GROUP : (h + 1) * HALF // LIST_GROUP]
            nc.vector.tensor_copy(out=key_words[h][:], in_=pool_words[:].bitcast(U32).indirect(half_offsets))
        quantize(1)

        neg_scores = [
            [psum.tile([P, HALF], F32, name="neg_scores%d%d" % (t, h)) for h in range(2)] for t in range(Q_TILES)
        ]
        for t in range(Q_TILES):
            for h in range(2):
                nc.tensor.matmul_mx(
                    out=neg_scores[t][h][:],
                    lhsT=q_codes[t][:].bitcast(FP8X4),
                    lhsT_scale=q_scales[t][:],
                    rhs=key_words[h][:].bitcast(FP8X4),
                    rhs_scale=key_scales[:].bitcast(U8)[:, h * HALF : (h + 1) * HALF],
                    start=True,
                    stop=True,
                )

        stats = [
            sb.tile([P, 2, BN_STATS], F32, name="stats0", align_bytes=64, tag="reused"),
            sb.tile([P, 2, BN_STATS], F32, name="stats1", align_bytes=64),
        ]
        mean_var = [sb.tile([P, 2], F32, name="mean_var%d" % t) for t in range(Q_TILES)]
        rstd = [sb.tile([P, 1], F32, name="rstd%d" % t) for t in range(Q_TILES)]
        for t in range(Q_TILES):
            for h in range(2):
                nc.vector.bn_stats(out=stats[t][:, h, :], in_=neg_scores[t][h][:])
            nc.vector.bn_aggr(out=mean_var[t][:], in_=stats[t][:].rearrange("p h s -> p (h s)"))

        centred = []
        for i, (t, start, width) in enumerate(PIECES):
            if start == 0:
                nc.scalar.activation(out=rstd[t][:], in_=mean_var[t][:, 1:2], func=ACT.Abs_reciprocal_sqrt, bias=EPS)
            piece = sb.tile([P, width], F32, name="centred%d" % i)
            source = neg_scores[t][start // HALF][:, start % HALF : start % HALF + width]
            nc.scalar.activation(out=piece[:], in_=source, func=ACT.Identity, scale=-1.0, bias=mean_var[t][:, 0:1])
            centred.append(piece)

        result = [sb.tile([P, N], F32, name="result%d" % t) for t in range(Q_TILES)]
        stored = 0
        for i, (t, start, width) in enumerate(PIECES):
            cols = slice(start, start + width)
            nc.vector.scalar_tensor_tensor(
                out=result[t][:, cols],
                in0=centred[i][:],
                scalar=rstd[t][:],
                in1=bm_sb[:, t, cols],
                op0=ALU.mult,
                op1=ALU.add,
            )
            if (t, start + width) in STORE_AFTER:
                run = slice(stored, start + width)
                nc.sync.dma_start(out=out[0, t * P : (t + 1) * P, run], in_=result[t][:, run])
                stored = (start + width) % N
